import numpy as np
import ml_dtypes


def mxq(x, axis, fmt="e4m3"):
    dtype, down = {"e4m3": (ml_dtypes.float8_e4m3fn, 7), "e5m2": (ml_dtypes.float8_e5m2, 14)}[fmt]
    v = np.moveaxis(np.asarray(x, np.float32).astype(ml_dtypes.bfloat16).astype(np.float64), axis, -1)
    blocks = v.reshape(v.shape[:-1] + (-1, 32))
    amax = np.abs(blocks).max(-1, keepdims=True)
    byte = np.maximum(np.where(amax > 0, np.frexp(amax)[1] - 1 + 127, 0) - down, 1)
    scale = np.exp2(byte - 127.0)
    codes = (blocks / scale).astype(np.float32).astype(dtype).astype(np.float64)
    return np.moveaxis((codes * scale).reshape(v.shape), -1, axis)


WIDE = False


def mx_kscale(k):
    if not WIDE:
        return np.ones(k)
    levels = np.array([10, -10, 5, -5, 0])
    if k % 512:
        return np.exp2(np.random.permutation(np.resize(levels, k // 32))).repeat(32)
    a = np.empty((k // 512, 16))
    for p in range(k // 512):
        a[p, :8] = np.random.permutation(np.resize(levels, 8))
        for g in range(8):
            far = levels[np.abs(levels - a[p, g]) >= 10]
            a[p, g + 8] = far[np.random.randint(len(far))]
    return np.exp2(a.ravel()).repeat(32)


def f64(x):
    return np.asarray(x).astype(np.float64)


def striped(idx):
    return np.tile(np.asarray(idx).reshape(-1, 16).T, (8, 1)).astype(np.uint16)


def unstriped(offs):
    return offs[:16].T.reshape(-1).astype(np.int64)


def striped8(idx):
    return np.asarray(idx).reshape(8, -1, 16).transpose(0, 2, 1).reshape(128, -1).astype(np.uint16)


def unstriped8(offs):
    return offs.reshape(8, 16, -1).transpose(0, 2, 1).reshape(8, -1).astype(np.int64)


def pick8(x, idx, run):
    r = np.arange(len(x))
    return x[r[:, None], idx[r % (8 * run) // run]]


E2M1 = np.array([0.0, 0.5, 1.0, 1.5, 2.0, 3.0, 4.0, 6.0, -0.0, -0.5, -1.0, -1.5, -2.0, -3.0, -4.0, -6.0])


def pack_weight(w, fmt):
    k, n = w.shape
    w = f64(np.asarray(w, np.float32).astype(ml_dtypes.bfloat16)).reshape(k // 32, 32, n)
    amax = np.abs(w).max(1)
    if fmt == "e4m3":
        byte = np.frexp(amax)[1] - 1 + 127 - 7
    else:
        mant, ex = np.frexp(amax / 6.0)
        byte = np.where(mant > 0.5, ex, ex - 1) + 127
    byte = np.clip(np.where(amax > 0, byte, 1), 1, 254)
    scaled = (w * np.exp2(127.0 - byte)[:, None, :]).reshape(k, n).astype(np.float32)
    by_word = np.ascontiguousarray(scaled.reshape(k // 512, 128, 4, n).transpose(0, 1, 3, 2))
    if fmt == "e4m3":
        words = by_word.astype(ml_dtypes.float8_e4m3fn).view(np.uint8)
    else:
        c = by_word.astype(ml_dtypes.float4_e2m1fn).view(np.uint8) & 0xF
        words = (c[..., 0::2] | (c[..., 1::2] << 4)).reshape(k // 512, 128, 2 * n)
    return np.ascontiguousarray(words), np.ascontiguousarray(byte.astype(np.uint8).reshape(k // 512, 16, n))


def unpack_weight(words, scales, fmt):
    g, _, n = scales.shape
    words = np.ascontiguousarray(words).reshape(g, 128, n, -1)
    if fmt == "e4m3":
        vals = words.view(ml_dtypes.float8_e4m3fn).astype(np.float64)
    else:
        nib = np.empty((g, 128, n, 4), np.uint8)
        nib[..., 0::2] = words & 0xF
        nib[..., 1::2] = words >> 4
        vals = E2M1[nib]
    vals = vals * np.repeat(np.exp2(scales.astype(np.float64) - 127.0), 8, axis=1)[..., None]
    return vals.transpose(0, 1, 3, 2).reshape(g * 512, n)


def sgn(shape):
    return np.random.uniform(0.5, 2.0, shape) * np.where(np.random.standard_normal(shape) < 0, -1.0, 1.0)


K, J, R, T, F, G, O, N = 512, 1024, 512, 2048, 1024, 1024, 512, 256


def setup_inputs():
    n = np.random.standard_normal
    idx = np.random.permutation(T)[:J]
    idx2 = np.stack([np.random.permutation(F)[:R] for _ in range(8)])
    idx3 = np.stack([np.random.permutation(G)[:R] for _ in range(8)])
    idx4 = np.stack([np.random.permutation(G)[:R] for _ in range(8)])
    idx5 = np.stack([np.random.permutation(J)[:O] for _ in range(8)])
    idx6 = np.stack([np.random.permutation(J)[:O] for _ in range(8)])
    idx7 = np.stack([np.random.permutation(J)[:O] for _ in range(8)])
    fk = mx_kscale(K)
    fr = mx_kscale(R)
    xtp = pack_weight(n((K, T)) * fk[:, None], "e2m1")
    wbp = pack_weight(n((R, N)) * 1 / np.sqrt(R) / fr[:, None], "e2m1")
    return {
        "xt_words": xtp[0],
        "xt_scales": xtp[1],
        "ua": (np.random.randint(-7, 8, (K, F)).astype(np.float64)).astype(np.float32),
        "ha": ((np.random.randint(8, 25, (K, 1)) / 1024.0) / fk[:, None]).astype(np.float32),
        "hb": (np.random.uniform(0.5, 1.6, (K, 1))).astype(np.float32),
        "sa": (sgn((R, 1)) * fr[:, None]).astype(np.float32),
        "sb": (sgn((R, 1)) * fr[:, None]).astype(np.float32),
        "sd": (sgn((R, 1)) * fr[:, None]).astype(np.float32),
        "wb_words": wbp[0],
        "wb_scales": wbp[1],
        "offs": striped(idx),
        "offs2": striped8(idx2),
        "offs3": striped8(idx3),
        "offs4": striped8(idx4),
        "offs5": striped8(idx5),
        "offs6": striped8(idx6),
        "offs7": striped8(idx7),
    }


def reference(xt_words, xt_scales, ua, ha, hb, sa, sb, sd, wb_words, wb_scales, offs, offs2, offs3, offs4, offs5, offs6, offs7):
    idx = unstriped(offs)
    idx2 = unstriped8(offs2)
    idx3 = unstriped8(offs3)
    idx4 = unstriped8(offs4)
    idx5 = unstriped8(offs5)
    idx6 = unstriped8(offs6)
    idx7 = unstriped8(offs7)
    xtu = unpack_weight(xt_words, xt_scales, "e2m1")
    wbu = unpack_weight(wb_words, wb_scales, "e2m1")
    wcd = pick8(f64(ua), idx2, 64) * f64(ha)
    wcp = np.zeros((K, G))
    wcp[np.arange(K)[:, None], idx3[np.arange(K) % 512 // 64]] = wcd
    wc = pick8(wcp, idx4, 64) * f64(hb)
    wcq = mxq(wc, 0, "e4m3")
    xtidxg = xtu[:, idx]
    a = wcq.T @ xtidxg
    hid = np.maximum(pick8(a, idx5, 64) * f64(sa) + pick8(a, idx6, 64) * f64(sb) + pick8(a, idx7, 64) * f64(sd), 0.0)
    hidq = mxq(hid, 0, "e4m3")
    y = wbu.T @ hidq
    return y

@@ -1,0 +1,219 @@
+from contextlib import ExitStack
+
+import concourse.mybir as mybir
+
+K, J, R, T, F, G, O, N = 512, 1024, 512, 2048, 1024, 1024, 512, 256
+FLOPS = 2 * K * R * J + 2 * R * N * O
+
+F32 = mybir.dt.float32
+BF16 = mybir.dt.bfloat16
+I32 = mybir.dt.int32
+U32 = mybir.dt.uint32
+U16 = mybir.dt.uint16
+U8 = mybir.dt.uint8
+FP8X4 = mybir.dt.float8_e4m3fn_x4
+FP4X4 = mybir.dt.float4_e2m1fn_x4
+COPY = mybir.ActivationFunctionType.Copy
+ADD = mybir.AluOpType.add
+
+P = 128
+PACK = 4
+BANK = 512
+LIST_COL = 16
+STAGE_ROW = 112
+
+
+def tile_picked_tokens_codepage_one_grouptriple_one_plain_kernel(
+    tc, xt_words, xt_scales, ua, ha, hb, sa, sb, sd, wb_words, wb_scales,
+    offs, offs2, offs3, offs4, offs5, offs6, offs7, out,
+):
+    nc = tc.nc
+    with ExitStack() as ctx:
+        lists = ctx.enter_context(tc.tile_pool(name="lists", bufs=1))
+        keep = ctx.enter_context(tc.tile_pool(name="keep", bufs=1))
+        shared = ctx.enter_context(tc.tile_pool(name="shared", bufs=1))
+        psum = ctx.enter_context(tc.psum_pool(name="psum", bufs=1))
+
+        def load_list(src, name):
+            t = lists.tile(list(src.shape), U16, name=name)
+            nc.sync.dma_start(t[:], src)
+            return t
+
+        def load_rows(src, name, queue):
+            t = keep.tile([P, PACK], F32, name=name)
+            queue.dma_start(t[:], src.rearrange("(p t) o -> p (t o)", t=PACK))
+            return t
+
+        ua_rows = ua.rearrange("(p t) f -> p t f", t=PACK)
+
+        def load_table(t):
+            tile = keep.tile([P, F], F32, name=f"ua{t}", tag=f"ua{t}", align_bytes=64)
+            nc.sync.dma_start(tile[:], ua_rows[:, t, :])
+            return tile
+
+        xs_win = keep.tile([P, T], U8, name="xs_win", align_bytes=64)
+        nc.vector.memset(xs_win[0:96, :].bitcast(I32), 0)
+        nc.vector.memset(xs_win[96:STAGE_ROW, :].bitcast(I32), 0)
+        ha_t = load_rows(ha, "ha_t", nc.scalar)
+        l_tok = load_list(offs, "l_tok")
+        nc.sync.dma_start(xs_win[STAGE_ROW:P, :].bitcast(I32), xt_scales[0].bitcast(I32))
+        l_code = load_list(offs2, "l_code")
+        tables = [load_table(0)]
+        l_put = load_list(offs3, "l_put")
+        tables.append(load_table(1))
+        l_read = load_list(offs4, "l_read")
+        hb_t = load_rows(hb, "hb_t", nc.sync)
+        tables.append(load_table(2))
+        tables.append(load_table(3))
+        xw_win = keep.tile([P, T], U16, name="xw_win", align_bytes=64)
+        nc.sync.dma_start(xw_win[:].bitcast(I32), xt_words[0].bitcast(I32))
+        l_slot = [load_list(src, f"l_slot{i}") for i, src in enumerate((offs5, offs6, offs7))]
+        slot_w = [load_rows(src, f"slot_w{i}", nc.sync) for i, src in enumerate((sa, sb, sd))]
+        wb_w = keep.tile([P, 2 * N], U8, name="wb_w", align_bytes=64)
+        nc.sync.dma_start(wb_w[:].bitcast(I32), wb_words[0].bitcast(I32))
+
+        pages = [keep.tile([P, G], F32, name=f"page{i}") for i in range(2)]
+        nc.vector.memset(pages[0][:], 0.0)
+        nc.gpsimd.memset(pages[1][:], 0.0)
+        wb_s = keep.tile([P, N], U8, name="wb_s", align_bytes=64)
+        nc.gpsimd.memset(wb_s[:].bitcast(I32), 0)
+        xs = keep.tile([P, J], U8, name="xs", align_bytes=64)
+        nc.gpsimd.memset(xs[:].bitcast(I32), 0)
+        for q in range(4):
+            nc.sync.dma_start(wb_s[32 * q : 32 * q + 4, :].bitcast(I32), wb_scales[0, 4 * q : 4 * q + 4, :].bitcast(I32))
+
+        xs_picked = keep.tile([P, J], U8, name="xs_picked", align_bytes=64)
+        nc.vector.tensor_copy(xs_picked[:], xs_win[:].indirect(l_tok[:]))
+        for q in range(4):
+            nc.sync.dma_start(
+                xs[32 * q : 32 * q + 4, :].bitcast(I32),
+                xs_picked[STAGE_ROW + 4 * q : STAGE_ROW + 4 * q + 4, :].bitcast(I32),
+            )
+
+        wcd = []
+        for t in range(PACK):
+            tile = keep.tile([P, R], F32, name=f"wcd{t}", tag=f"wcd{t}", align_bytes=64)
+            pieces = 2 if t == 0 else 1
+            w = R // pieces
+            for h in range(pieces):
+                nc.scalar.activation(
+                    tile[:, h * w : (h + 1) * w],
+                    tables[t][:].indirect(l_code[:, h * w // LIST_COL : (h + 1) * w // LIST_COL]),
+                    COPY,
+                    scale=ha_t[:, t : t + 1],
+                )
+            wcd.append(tile)
+
+        wc = keep.tile([P, PACK, R], BF16, name="wc", tag=f"ua{PACK - 1}", align_bytes=64)
+        for t in range(PACK):
+            page = pages[t % 2]
+            pieces = 2 if t == 0 else 1
+            w = R // pieces
+            for h in range(pieces):
+                nc.vector.tensor_copy(
+                    page[:].indirect(l_put[:, h * w // LIST_COL : (h + 1) * w // LIST_COL]),
+                    wcd[t][:, h * w : (h + 1) * w],
+                )
+            nc.scalar.activation(wc[:, t, :], page[:].indirect(l_read[:]), COPY, scale=hb_t[:, t : t + 1])
+
+        QUART = J // 4
+        xw_head = keep.tile([P, 3 * QUART], U16, name="xw_head", tag=f"wcd{PACK - 1}", align_bytes=64)
+        for lo, hi in ((0, 2 * QUART), (2 * QUART, 3 * QUART)):
+            nc.vector.tensor_copy(xw_head[:, lo:hi], xw_win[:].indirect(l_tok[:, lo // LIST_COL : hi // LIST_COL]))
+
+        wc_dealt = wc[:].rearrange("p j (m t) -> p t m j", t=PACK)
+        banks = [0]
+
+        def next_bank(width, name):
+            acc = psum.tile([P, width], F32, name=name, tag=f"bank{banks[0] % 8}")
+            banks[0] = banks[0] + 1
+            return acc
+
+        def quantise_matrix(t):
+            grouped = shared.tile([P, P, PACK], BF16, name=f"wc_g{t}", align_bytes=64, offset=0 if t == 0 else 2 * QUART)
+            if t == 0:
+                nc.scalar.copy(grouped[:], wc_dealt[:, t, :, :])
+            else:
+                nc.vector.tensor_copy(grouped[:], wc_dealt[:, t, :, :])
+            codes = keep.tile([P, P], U32, name=f"wc_c{t}", align_bytes=64)
+            scales = keep.tile([P, P], U8, name=f"wc_s{t}", align_bytes=64)
+            nc.vector.quantize_mx(codes[:].bitcast(FP8X4), scales[:], grouped[:].rearrange("p m j -> p (m j)"))
+            return codes, scales
+
+        matrix = [quantise_matrix(0)]
+        xw_last = shared.tile([P, QUART], U16, name="xw_last", align_bytes=64, offset=0)
+        nc.vector.tensor_copy(xw_last[:], xw_win[:].indirect(l_tok[:, 3 * QUART // LIST_COL :]))
+
+        def words(lo, hi):
+            return xw_last[:] if lo == 3 * QUART else xw_head[:, lo:hi]
+
+        a_tiles = []
+        for t in range(PACK):
+            if t > 0:
+                matrix.append(quantise_matrix(t))
+            codes, scales = matrix[t]
+            a_t = keep.tile([P, J], F32, name=f"a{t}")
+            if t == 0:
+                groups = [[(q * QUART, (q + 1) * QUART)] for q in range(4)]
+            else:
+                groups = [[(0, 2 * QUART)], [(2 * QUART, 3 * QUART), (3 * QUART, J)]]
+            for spans in groups:
+                first, last = spans[0][0], spans[-1][1]
+                acc = next_bank(last - first, f"acc{t}_{first}")
+                for lo, hi in spans:
+                    nc.tensor.matmul_mx(
+                        acc[:, lo - first : hi - first], lhsT=codes[:].bitcast(FP8X4), lhsT_scale=scales[:],
+                        rhs=words(lo, hi).bitcast(FP4X4), rhs_scale=xs[:, lo:hi], start=True, stop=True,
+                    )
+                if t == 0:
+                    nc.scalar.copy(a_t[:, first:last], acc[:])
+                else:
+                    nc.vector.tensor_copy(a_t[:, first:last], acc[:])
+            a_tiles.append(a_t)
+
+        hid = keep.tile([P, PACK, O], BF16, name="hid", align_bytes=64)
+        HALF = O // 2
+
+        def neighbours(t, lo, hi):
+            g = []
+            for i in range(3):
+                gi = keep.tile([P, hi - lo], F32, name=f"g{t}_{lo}_{i}")
+                nc.scalar.activation(
+                    gi[:], a_tiles[t][:].indirect(l_slot[i][:, lo // LIST_COL : hi // LIST_COL]),
+                    COPY, scale=slot_w[i][:, t : t + 1],
+                )
+                g.append(gi)
+                if i == 1:
+                    part = keep.tile([P, hi - lo], F32, name=f"part{t}_{lo}", tag="part", align_bytes=64)
+                    nc.vector.tensor_tensor(part[:], g[0][:], g[1][:], ADD)
+            nc.vector.tensor_tensor(hid[:, t, lo:hi], part[:], g[2][:], ADD)
+
+        def second_product(h):
+            lo, hi = h * HALF, (h + 1) * HALF
+            grouped = keep.tile([P, HALF, PACK], BF16, name=f"hid_g{h}", tag="part", align_bytes=64)
+            nc.vector.tensor_scalar_max(
+                grouped[:].rearrange("p (c i) t -> p c t i", i=4),
+                hid[:, :, lo:hi].rearrange("p t (c i) -> p c t i", i=4),
+                0.0,
+            )
+            codes = keep.tile([P, HALF], U32, name=f"hid_c{h}", align_bytes=64)
+            scales = keep.tile([P, HALF], U8, name=f"hid_s{h}", align_bytes=64)
+            nc.vector.quantize_mx(codes[:].bitcast(FP8X4), scales[:], grouped[:].rearrange("p o t -> p (o t)"))
+            for b in range(N // P):
+                acc = next_bank(HALF, f"y{h}_{b}")
+                nc.tensor.matmul_mx(
+                    acc[:], lhsT=wb_w[:, 2 * P * b : 2 * P * (b + 1)].bitcast(FP4X4), lhsT_scale=wb_s[:, P * b : P * (b + 1)],
+                    rhs=codes[:].bitcast(FP8X4), rhs_scale=scales[:], start=True, stop=True,
+                )
+                y = keep.tile([P, HALF], F32, name=f"y_sb{h}_{b}")
+                if h == 0 or b == 0:
+                    nc.scalar.copy(y[:], acc[:])
+                else:
+                    nc.vector.tensor_copy(y[:], acc[:])
+                nc.sync.dma_start(out[P * b : P * (b + 1), lo:hi], y[:])
+
+        for t in range(PACK - 1):
+            neighbours(t, 0, O)
+        for h in range(2):
+            neighbours(PACK - 1, h * HALF, (h + 1) * HALF)
+            second_product(h)

@@ -55,6 +55,9 @@ def tile_picked_tokens_codepage_one_grouptriple_one_plain_kernel(
         nc.vector.memset(xs_win[0:96, :].bitcast(I32), 0)
         nc.vector.memset(xs_win[96:STAGE_ROW, :].bitcast(I32), 0)
         ha_t = load_rows(ha, "ha_t", nc.scalar)
+        warm = keep.tile([P, 2], F32, name="warm")
+        nc.gpsimd.memset(warm[:, 0:1], 0.0)
+        nc.scalar.activation(warm[:, 1:2], warm[:, 0:1], COPY)
         l_tok = load_list(offs, "l_tok")
         nc.sync.dma_start(xs_win[STAGE_ROW:P, :].bitcast(I32), xt_scales[0].bitcast(I32))
         l_code = load_list(offs2, "l_code")
@@ -73,7 +76,7 @@ def tile_picked_tokens_codepage_one_grouptriple_one_plain_kernel(
         nc.sync.dma_start(wb_w[:].bitcast(I32), wb_words[0].bitcast(I32))
 
         pages = [keep.tile([P, G], F32, name=f"page{i}") for i in range(2)]
-        nc.vector.memset(pages[0][:], 0.0)
+        nc.gpsimd.memset(pages[0][:], 0.0)
         nc.gpsimd.memset(pages[1][:], 0.0)
         wb_s = keep.tile([P, N], U8, name="wb_s", align_bytes=64)
         nc.gpsimd.memset(wb_s[:].bitcast(I32), 0)
@@ -114,38 +117,53 @@ def tile_picked_tokens_codepage_one_grouptriple_one_plain_kernel(
                     page[:].indirect(l_put[:, h * w // LIST_COL : (h + 1) * w // LIST_COL]),
                     wcd[t][:, h * w : (h + 1) * w],
                 )
-            nc.scalar.activation(wc[:, t, :], page[:].indirect(l_read[:]), COPY, scale=hb_t[:, t : t + 1])
+            pieces = 2 if t == PACK - 1 else 1
+            w = R // pieces
+            for h in range(pieces):
+                nc.scalar.activation(
+                    wc[:, t, h * w : (h + 1) * w],
+                    page[:].indirect(l_read[:, h * w // LIST_COL : (h + 1) * w // LIST_COL]),
+                    COPY,
+                    scale=hb_t[:, t : t + 1],
+                )
 
         QUART = J // 4
-        xw_head = keep.tile([P, 3 * QUART], U16, name="xw_head", tag=f"wcd{PACK - 1}", align_bytes=64)
-        for lo, hi in ((0, 2 * QUART), (2 * QUART, 3 * QUART)):
-            nc.vector.tensor_copy(xw_head[:, lo:hi], xw_win[:].indirect(l_tok[:, lo // LIST_COL : hi // LIST_COL]))
+        xw_head = keep.tile([P, 2 * QUART], U16, name="xw_head", tag=f"wcd{PACK - 1}", align_bytes=64)
+        nc.vector.tensor_copy(xw_head[:], xw_win[:].indirect(l_tok[:, : 2 * QUART // LIST_COL]))
 
         wc_dealt = wc[:].rearrange("p j (m t) -> p t m j", t=PACK)
         banks = [0]
 
-        def next_bank(width, name):
-            acc = psum.tile([P, width], F32, name=name, tag=f"bank{banks[0] % 8}")
+        def next_bank(shape, name):
+            acc = psum.tile(shape, F32, name=name, tag=f"bank{banks[0] % 8}")
             banks[0] = banks[0] + 1
             return acc
 
         def quantise_matrix(t):
-            grouped = shared.tile([P, P, PACK], BF16, name=f"wc_g{t}", align_bytes=64, offset=0 if t == 0 else 2 * QUART)
+            grouped = shared.tile([P, P, PACK], BF16, name=f"wc_g{t}", align_bytes=64, offset=512 if t == 0 else 1536)
+            pieces = 2 if t == 0 else 1
+            w = P // pieces
+            for h in range(pieces):
+                nc.vector.tensor_copy(grouped[:, h * w : (h + 1) * w, :], wc_dealt[:, t, h * w : (h + 1) * w, :])
             if t == 0:
-                nc.scalar.copy(grouped[:], wc_dealt[:, t, :, :])
+                codes = shared.tile([P, P], U32, name=f"wc_c{t}", align_bytes=64, offset=1536)
             else:
-                nc.vector.tensor_copy(grouped[:], wc_dealt[:, t, :, :])
-            codes = keep.tile([P, P], U32, name=f"wc_c{t}", align_bytes=64)
+                codes = keep.tile([P, P], U32, name=f"wc_c{t}", tag="part" if t == PACK - 1 else f"wc_c{t}", align_bytes=64)
             scales = keep.tile([P, P], U8, name=f"wc_s{t}", align_bytes=64)
             nc.vector.quantize_mx(codes[:].bitcast(FP8X4), scales[:], grouped[:].rearrange("p m j -> p (m j)"))
             return codes, scales
 
         matrix = [quantise_matrix(0)]
-        xw_last = shared.tile([P, QUART], U16, name="xw_last", align_bytes=64, offset=0)
-        nc.vector.tensor_copy(xw_last[:], xw_win[:].indirect(l_tok[:, 3 * QUART // LIST_COL :]))
+        xw_tail = shared.tile([P, 2 * QUART], U16, name="xw_tail", align_bytes=64, offset=0)
+        for q in range(2):
+            lo = (2 + q) * QUART
+            nc.vector.tensor_copy(
+                xw_tail[:, q * QUART : (q + 1) * QUART],
+                xw_win[:].indirect(l_tok[:, lo // LIST_COL : (lo + QUART) // LIST_COL]),
+            )
 
         def words(lo, hi):
-            return xw_last[:] if lo == 3 * QUART else xw_head[:, lo:hi]
+            return xw_head[:, lo:hi] if hi <= 2 * QUART else xw_tail[:, lo - 2 * QUART : hi - 2 * QUART]
 
         a_tiles = []
         for t in range(PACK):
@@ -153,67 +171,82 @@ def tile_picked_tokens_codepage_one_grouptriple_one_plain_kernel(
                 matrix.append(quantise_matrix(t))
             codes, scales = matrix[t]
             a_t = keep.tile([P, J], F32, name=f"a{t}")
-            if t == 0:
-                groups = [[(q * QUART, (q + 1) * QUART)] for q in range(4)]
-            else:
-                groups = [[(0, 2 * QUART)], [(2 * QUART, 3 * QUART), (3 * QUART, J)]]
-            for spans in groups:
-                first, last = spans[0][0], spans[-1][1]
-                acc = next_bank(last - first, f"acc{t}_{first}")
-                for lo, hi in spans:
-                    nc.tensor.matmul_mx(
-                        acc[:, lo - first : hi - first], lhsT=codes[:].bitcast(FP8X4), lhsT_scale=scales[:],
-                        rhs=words(lo, hi).bitcast(FP4X4), rhs_scale=xs[:, lo:hi], start=True, stop=True,
-                    )
-                if t == 0:
-                    nc.scalar.copy(a_t[:, first:last], acc[:])
+            width = QUART if t == 0 else BANK
+            for lo in range(0, J, width):
+                hi = lo + width
+                acc = next_bank([P, width], f"acc{t}_{lo}")
+                nc.tensor.matmul_mx(
+                    acc[:], lhsT=codes[:].bitcast(FP8X4), lhsT_scale=scales[:],
+                    rhs=words(lo, hi).bitcast(FP4X4), rhs_scale=xs[:, lo:hi], start=True, stop=True,
+                )
+                if t == 0 and lo != 2 * QUART:
+                    nc.scalar.copy(a_t[:, lo:hi], acc[:])
                 else:
-                    nc.vector.tensor_copy(a_t[:, first:last], acc[:])
+                    nc.vector.tensor_copy(a_t[:, lo:hi], acc[:])
             a_tiles.append(a_t)
 
         hid = keep.tile([P, PACK, O], BF16, name="hid", align_bytes=64)
         HALF = O // 2
+        out_rows = out.rearrange("(b p) o -> p b o", p=P)
 
-        def neighbours(t, lo, hi):
+        def neighbours(t, lo, hi, part_tag, pieces):
             g = []
             for i in range(3):
-                gi = keep.tile([P, hi - lo], F32, name=f"g{t}_{lo}_{i}")
+                shares = (t, lo) in ((3, 0), (2, HALF))
+                gi = keep.tile([P, hi - lo], F32, name=f"g{t}_{lo}_{i}", tag=f"g_shared{i}" if shares else f"g{t}_{lo}_{i}")
                 nc.scalar.activation(
                     gi[:], a_tiles[t][:].indirect(l_slot[i][:, lo // LIST_COL : hi // LIST_COL]),
                     COPY, scale=slot_w[i][:, t : t + 1],
                 )
                 g.append(gi)
                 if i == 1:
-                    part = keep.tile([P, hi - lo], F32, name=f"part{t}_{lo}", tag="part", align_bytes=64)
+                    part = keep.tile([P, hi - lo], F32, name=f"part{t}_{lo}", tag=part_tag, align_bytes=64)
                     nc.vector.tensor_tensor(part[:], g[0][:], g[1][:], ADD)
-            nc.vector.tensor_tensor(hid[:, t, lo:hi], part[:], g[2][:], ADD)
+            w = (hi - lo) // pieces
+            for s in range(0, hi - lo, w):
+                nc.vector.tensor_tensor(hid[:, t, lo + s : lo + s + w], part[:, s : s + w], g[2][:, s : s + w], ADD)
 
-        def second_product(h):
-            lo, hi = h * HALF, (h + 1) * HALF
-            grouped = keep.tile([P, HALF, PACK], BF16, name=f"hid_g{h}", tag="part", align_bytes=64)
+        def interleave_hidden(lo, hi, tag):
+            grouped = keep.tile([P, hi - lo, PACK], BF16, name=f"hid_g{lo}", tag=tag, align_bytes=64)
             nc.vector.tensor_scalar_max(
                 grouped[:].rearrange("p (c i) t -> p c t i", i=4),
                 hid[:, :, lo:hi].rearrange("p t (c i) -> p c t i", i=4),
                 0.0,
             )
-            codes = keep.tile([P, HALF], U32, name=f"hid_c{h}", align_bytes=64)
-            scales = keep.tile([P, HALF], U8, name=f"hid_s{h}", align_bytes=64)
+            return grouped
+
+        def quantise_hidden(grouped, lo, tag):
+            width = grouped.shape[1]
+            codes = keep.tile([P, width], U32, name=f"hid_c{lo}", tag=tag, align_bytes=64)
+            scales = keep.tile([P, width], U8, name=f"hid_s{lo}", align_bytes=64)
             nc.vector.quantize_mx(codes[:].bitcast(FP8X4), scales[:], grouped[:].rearrange("p o t -> p (o t)"))
+            return codes, scales
+
+        def second_product(codes, scales, lo, engines):
+            width = codes.shape[1]
+            y = keep.tile([P, N // P, width], F32, name=f"y_sb{lo}")
             for b in range(N // P):
-                acc = next_bank(HALF, f"y{h}_{b}")
+                acc = next_bank([P, width], f"y{lo}_{b}")
                 nc.tensor.matmul_mx(
                     acc[:], lhsT=wb_w[:, 2 * P * b : 2 * P * (b + 1)].bitcast(FP4X4), lhsT_scale=wb_s[:, P * b : P * (b + 1)],
                     rhs=codes[:].bitcast(FP8X4), rhs_scale=scales[:], start=True, stop=True,
                 )
-                y = keep.tile([P, HALF], F32, name=f"y_sb{h}_{b}")
-                if h == 0 or b == 0:
-                    nc.scalar.copy(y[:], acc[:])
+                if engines[b] == "scalar":
+                    nc.scalar.copy(y[:, b, :], acc[:])
                 else:
-                    nc.vector.tensor_copy(y[:], acc[:])
-                nc.sync.dma_start(out[P * b : P * (b + 1), lo:hi], y[:])
+                    nc.vector.tensor_copy(y[:, b, :], acc[:])
+            nc.sync.dma_start(out_rows[:, :, lo : lo + width], y[:])
 
-        for t in range(PACK - 1):
-            neighbours(t, 0, O)
-        for h in range(2):
-            neighbours(PACK - 1, h * HALF, (h + 1) * HALF)
-            second_product(h)
+        neighbours(0, 0, O, "part", 1)
+        neighbours(1, 0, O, "part", 1)
+        neighbours(2, 0, HALF, "part", 1)
+        neighbours(3, 0, HALF, "part", 1)
+        codes, scales = quantise_hidden(interleave_hidden(0, HALF, "part"), 0, "codes0")
+        second_product(codes, scales, 0, ("scalar", "scalar"))
+        neighbours(3, HALF, O, "part", 1)
+        neighbours(2, HALF, O, "part", 2)
+        starts = (HALF, HALF + HALF // 2)
+        grouped = [interleave_hidden(lo, lo + HALF // 2, f"hid_g{lo}") for lo in starts]
+        quantised = [quantise_hidden(g, lo, f"codes{lo}") for g, lo in zip(grouped, starts)]
+        second_product(*quantised[0], starts[0], ("scalar", "scalar"))
+        second_product(*quantised[1], starts[1], ("scalar", "vector"))

@@ -76,8 +76,8 @@ def tile_picked_tokens_codepage_one_grouptriple_one_plain_kernel(
         nc.sync.dma_start(wb_w[:].bitcast(I32), wb_words[0].bitcast(I32))
 
         pages = [keep.tile([P, G], F32, name=f"page{i}") for i in range(2)]
-        nc.gpsimd.memset(pages[0][:], 0.0)
-        nc.gpsimd.memset(pages[1][:], 0.0)
+        nc.vector.memset(pages[0][:], 0.0)
+        nc.vector.memset(pages[1][:], 0.0)
         wb_s = keep.tile([P, N], U8, name="wb_s", align_bytes=64)
         nc.gpsimd.memset(wb_s[:].bitcast(I32), 0)
         xs = keep.tile([P, J], U8, name="xs", align_bytes=64)

@@ -54,12 +54,12 @@ def tile_picked_tokens_codepage_one_grouptriple_one_plain_kernel(
         xs_win = keep.tile([P, T], U8, name="xs_win", align_bytes=64)
         nc.vector.memset(xs_win[0:96, :].bitcast(I32), 0)
         nc.vector.memset(xs_win[96:STAGE_ROW, :].bitcast(I32), 0)
+        nc.scalar.dma_start(xs_win[STAGE_ROW:P, :].bitcast(I32), xt_scales[0].bitcast(I32))
         ha_t = load_rows(ha, "ha_t", nc.scalar)
         warm = keep.tile([P, 2], F32, name="warm")
         nc.gpsimd.memset(warm[:, 0:1], 0.0)
         nc.scalar.activation(warm[:, 1:2], warm[:, 0:1], COPY)
         l_tok = load_list(offs, "l_tok")
-        nc.sync.dma_start(xs_win[STAGE_ROW:P, :].bitcast(I32), xt_scales[0].bitcast(I32))
         l_code = load_list(offs2, "l_code")
         tables = [load_table(0)]
         l_put = load_list(offs3, "l_put")
@@ -96,27 +96,13 @@ def tile_picked_tokens_codepage_one_grouptriple_one_plain_kernel(
         wcd = []
         for t in range(PACK):
             tile = keep.tile([P, R], F32, name=f"wcd{t}", tag=f"wcd{t}", align_bytes=64)
-            pieces = 2 if t == 0 else 1
-            w = R // pieces
-            for h in range(pieces):
-                nc.scalar.activation(
-                    tile[:, h * w : (h + 1) * w],
-                    tables[t][:].indirect(l_code[:, h * w // LIST_COL : (h + 1) * w // LIST_COL]),
-                    COPY,
-                    scale=ha_t[:, t : t + 1],
-                )
+            nc.scalar.activation(tile[:], tables[t][:].indirect(l_code[:]), COPY, scale=ha_t[:, t : t + 1])
             wcd.append(tile)
 
         wc = keep.tile([P, PACK, R], BF16, name="wc", tag=f"ua{PACK - 1}", align_bytes=64)
         for t in range(PACK):
             page = pages[t % 2]
-            pieces = 2 if t == 0 else 1
-            w = R // pieces
-            for h in range(pieces):
-                nc.vector.tensor_copy(
-                    page[:].indirect(l_put[:, h * w // LIST_COL : (h + 1) * w // LIST_COL]),
-                    wcd[t][:, h * w : (h + 1) * w],
-                )
+            nc.vector.tensor_copy(page[:].indirect(l_put[:]), wcd[t][:])
             pieces = 2 if t == PACK - 1 else 1
             w = R // pieces
             for h in range(pieces):
@@ -131,7 +117,7 @@ def tile_picked_tokens_codepage_one_grouptriple_one_plain_kernel(
         xw_head = keep.tile([P, 2 * QUART], U16, name="xw_head", tag=f"wcd{PACK - 1}", align_bytes=64)
         nc.vector.tensor_copy(xw_head[:], xw_win[:].indirect(l_tok[:, : 2 * QUART // LIST_COL]))
 
-        wc_dealt = wc[:].rearrange("p j (m t) -> p t m j", t=PACK)
+        wc_dealt = wc[:].rearrange("p j (c i t) -> p t c j i", i=2, t=PACK)
         banks = [0]
 
         def next_bank(shape, name):
@@ -142,14 +128,15 @@ def tile_picked_tokens_codepage_one_grouptriple_one_plain_kernel(
         def quantise_matrix(t):
             grouped = shared.tile([P, P, PACK], BF16, name=f"wc_g{t}", align_bytes=64, offset=512 if t == 0 else 1536)
             pieces = 2 if t == 0 else 1
-            w = P // pieces
+            w = P // 2 // pieces
+            walk = grouped[:].rearrange("p (c i) j -> p c j i", i=2)
             for h in range(pieces):
-                nc.vector.tensor_copy(grouped[:, h * w : (h + 1) * w, :], wc_dealt[:, t, h * w : (h + 1) * w, :])
+                nc.vector.tensor_copy(walk[:, h * w : (h + 1) * w], wc_dealt[:, t, h * w : (h + 1) * w])
             if t == 0:
                 codes = shared.tile([P, P], U32, name=f"wc_c{t}", align_bytes=64, offset=1536)
             else:
-                codes = keep.tile([P, P], U32, name=f"wc_c{t}", tag="part" if t == PACK - 1 else f"wc_c{t}", align_bytes=64)
-            scales = keep.tile([P, P], U8, name=f"wc_s{t}", align_bytes=64)
+                codes = keep.tile([P, P], U32, name=f"wc_c{t}", tag="part_a" if t == PACK - 1 else f"wc_c{t}", align_bytes=64)
+            scales = keep.tile([P, P], U8, name=f"wc_s{t}", tag="part_b" if t == PACK - 1 else f"wc_s{t}", align_bytes=64)
             nc.vector.quantize_mx(codes[:].bitcast(FP8X4), scales[:], grouped[:].rearrange("p m j -> p (m j)"))
             return codes, scales
 
@@ -225,6 +212,7 @@ def tile_picked_tokens_codepage_one_grouptriple_one_plain_kernel(
         def second_product(codes, scales, lo, engines):
             width = codes.shape[1]
             y = keep.tile([P, N // P, width], F32, name=f"y_sb{lo}")
+            last = lo + width == O
             for b in range(N // P):
                 acc = next_bank([P, width], f"y{lo}_{b}")
                 nc.tensor.matmul_mx(
@@ -235,16 +223,20 @@ def tile_picked_tokens_codepage_one_grouptriple_one_plain_kernel(
                     nc.scalar.copy(y[:, b, :], acc[:])
                 else:
                     nc.vector.tensor_copy(y[:, b, :], acc[:])
-            nc.sync.dma_start(out_rows[:, :, lo : lo + width], y[:])
+                if last:
+                    queue = nc.scalar if engines[b] == "scalar" else nc.sync
+                    queue.dma_start(out_rows[:, b, lo : lo + width], y[:, b, :])
+            if not last:
+                nc.sync.dma_start(out_rows[:, :, lo : lo + width], y[:])
 
-        neighbours(0, 0, O, "part", 1)
-        neighbours(1, 0, O, "part", 1)
-        neighbours(2, 0, HALF, "part", 1)
-        neighbours(3, 0, HALF, "part", 1)
-        codes, scales = quantise_hidden(interleave_hidden(0, HALF, "part"), 0, "codes0")
+        neighbours(0, 0, O, "part_a", 1)
+        neighbours(1, 0, O, "part_b", 1)
+        neighbours(2, 0, HALF, "part_a", 1)
+        neighbours(3, 0, HALF, "part_b", 1)
+        codes, scales = quantise_hidden(interleave_hidden(0, HALF, "hid_g0"), 0, "codes0")
         second_product(codes, scales, 0, ("scalar", "scalar"))
-        neighbours(3, HALF, O, "part", 1)
-        neighbours(2, HALF, O, "part", 2)
+        neighbours(3, HALF, O, "part_a", 1)
+        neighbours(2, HALF, O, "part_b", 2)
         starts = (HALF, HALF + HALF // 2)
         grouped = [interleave_hidden(lo, lo + HALF // 2, f"hid_g{lo}") for lo in starts]
         quantised = [quantise_hidden(g, lo, f"codes{lo}") for g, lo in zip(grouped, starts)]

from contextlib import ExitStack

import concourse.mybir as mybir

K, J, R, T, F, G, O, N = 512, 1024, 512, 2048, 1024, 1024, 512, 256
FLOPS = 2 * K * R * J + 2 * R * N * O

F32 = mybir.dt.float32
BF16 = mybir.dt.bfloat16
I32 = mybir.dt.int32
U32 = mybir.dt.uint32
U16 = mybir.dt.uint16
U8 = mybir.dt.uint8
FP8X4 = mybir.dt.float8_e4m3fn_x4
FP4X4 = mybir.dt.float4_e2m1fn_x4
COPY = mybir.ActivationFunctionType.Copy
ADD = mybir.AluOpType.add

P = 128
PACK = 4
BANK = 512
LIST_COL = 16
STAGE_ROW = 112


def tile_picked_tokens_codepage_one_grouptriple_one_plain_kernel(
    tc, xt_words, xt_scales, ua, ha, hb, sa, sb, sd, wb_words, wb_scales,
    offs, offs2, offs3, offs4, offs5, offs6, offs7, out,
):
    nc = tc.nc
    with ExitStack() as ctx:
        lists = ctx.enter_context(tc.tile_pool(name="lists", bufs=1))
        keep = ctx.enter_context(tc.tile_pool(name="keep", bufs=1))
        shared = ctx.enter_context(tc.tile_pool(name="shared", bufs=1))
        psum = ctx.enter_context(tc.psum_pool(name="psum", bufs=1))

        def load_list(src, name):
            t = lists.tile(list(src.shape), U16, name=name)
            nc.sync.dma_start(t[:], src)
            return t

        def load_rows(src, name, queue):
            t = keep.tile([P, PACK], F32, name=name)
            queue.dma_start(t[:], src.rearrange("(p t) o -> p (t o)", t=PACK))
            return t

        ua_rows = ua.rearrange("(p t) f -> p t f", t=PACK)

        def load_table(t):
            tile = keep.tile([P, F], F32, name=f"ua{t}", tag=f"ua{t}", align_bytes=64)
            nc.sync.dma_start(tile[:], ua_rows[:, t, :])
            return tile

        xs_win = keep.tile([P, T], U8, name="xs_win", align_bytes=64)
        nc.vector.memset(xs_win[0:96, :].bitcast(I32), 0)
        nc.vector.memset(xs_win[96:STAGE_ROW, :].bitcast(I32), 0)
        nc.scalar.dma_start(xs_win[STAGE_ROW:P, :].bitcast(I32), xt_scales[0].bitcast(I32))
        ha_t = load_rows(ha, "ha_t", nc.scalar)
        warm = keep.tile([P, 2], F32, name="warm")
        nc.gpsimd.memset(warm[:, 0:1], 0.0)
        nc.scalar.activation(warm[:, 1:2], warm[:, 0:1], COPY)
        l_tok = load_list(offs, "l_tok")
        l_code = load_list(offs2, "l_code")
        tables = [load_table(0)]
        l_put = load_list(offs3, "l_put")
        tables.append(load_table(1))
        l_read = load_list(offs4, "l_read")
        hb_t = load_rows(hb, "hb_t", nc.sync)
        tables.append(load_table(2))
        tables.append(load_table(3))
        xw_win = keep.tile([P, T], U16, name="xw_win", align_bytes=64)
        nc.sync.dma_start(xw_win[:].bitcast(I32), xt_words[0].bitcast(I32))
        l_slot = [load_list(src, f"l_slot{i}") for i, src in enumerate((offs5, offs6, offs7))]
        slot_w = [load_rows(src, f"slot_w{i}", nc.sync) for i, src in enumerate((sa, sb, sd))]
        wb_w = keep.tile([P, 2 * N], U8, name="wb_w", align_bytes=64)
        nc.sync.dma_start(wb_w[:].bitcast(I32), wb_words[0].bitcast(I32))

        pages = [keep.tile([P, G], F32, name=f"page{i}") for i in range(2)]
        nc.vector.memset(pages[0][:], 0.0)
        nc.vector.memset(pages[1][:], 0.0)
        wb_s = keep.tile([P, N], U8, name="wb_s", align_bytes=64)
        nc.gpsimd.memset(wb_s[:].bitcast(I32), 0)
        xs = keep.tile([P, J], U8, name="xs", align_bytes=64)
        nc.gpsimd.memset(xs[:].bitcast(I32), 0)
        for q in range(4):
            nc.sync.dma_start(wb_s[32 * q : 32 * q + 4, :].bitcast(I32), wb_scales[0, 4 * q : 4 * q + 4, :].bitcast(I32))

        xs_picked = keep.tile([P, J], U8, name="xs_picked", align_bytes=64)
        nc.vector.tensor_copy(xs_picked[:], xs_win[:].indirect(l_tok[:]))
        for q in range(4):
            nc.sync.dma_start(
                xs[32 * q : 32 * q + 4, :].bitcast(I32),
                xs_picked[STAGE_ROW + 4 * q : STAGE_ROW + 4 * q + 4, :].bitcast(I32),
            )

        wcd = []
        for t in range(PACK):
            tile = keep.tile([P, R], F32, name=f"wcd{t}", tag=f"wcd{t}", align_bytes=64)
            nc.scalar.activation(tile[:], tables[t][:].indirect(l_code[:]), COPY, scale=ha_t[:, t : t + 1])
            wcd.append(tile)

        wc = keep.tile([P, PACK, R], BF16, name="wc", tag=f"ua{PACK - 1}", align_bytes=64)
        for t in range(PACK):
            page = pages[t % 2]
            nc.vector.tensor_copy(page[:].indirect(l_put[:]), wcd[t][:])
            pieces = 2 if t == PACK - 1 else 1
            w = R // pieces
            for h in range(pieces):
                nc.scalar.activation(
                    wc[:, t, h * w : (h + 1) * w],
                    page[:].indirect(l_read[:, h * w // LIST_COL : (h + 1) * w // LIST_COL]),
                    COPY,
                    scale=hb_t[:, t : t + 1],
                )

        QUART = J // 4
        xw_head = keep.tile([P, 2 * QUART], U16, name="xw_head", tag=f"wcd{PACK - 1}", align_bytes=64)
        nc.vector.tensor_copy(xw_head[:], xw_win[:].indirect(l_tok[:, : 2 * QUART // LIST_COL]))

        wc_dealt = wc[:].rearrange("p j (c i t) -> p t c j i", i=2, t=PACK)
        banks = [0]

        def next_bank(shape, name):
            acc = psum.tile(shape, F32, name=name, tag=f"bank{banks[0] % 8}")
            banks[0] = banks[0] + 1
            return acc

        def quantise_matrix(t):
            grouped = shared.tile([P, P, PACK], BF16, name=f"wc_g{t}", align_bytes=64, offset=512 if t == 0 else 1536)
            pieces = 2 if t == 0 else 1
            w = P // 2 // pieces
            walk = grouped[:].rearrange("p (c i) j -> p c j i", i=2)
            for h in range(pieces):
                nc.vector.tensor_copy(walk[:, h * w : (h + 1) * w], wc_dealt[:, t, h * w : (h + 1) * w])
            if t == 0:
                codes = shared.tile([P, P], U32, name=f"wc_c{t}", align_bytes=64, offset=1536)
            else:
                codes = keep.tile([P, P], U32, name=f"wc_c{t}", tag="part_a" if t == PACK - 1 else f"wc_c{t}", align_bytes=64)
            scales = keep.tile([P, P], U8, name=f"wc_s{t}", tag="part_b" if t == PACK - 1 else f"wc_s{t}", align_bytes=64)
            nc.vector.quantize_mx(codes[:].bitcast(FP8X4), scales[:], grouped[:].rearrange("p m j -> p (m j)"))
            return codes, scales

        matrix = [quantise_matrix(0)]
        xw_tail = shared.tile([P, 2 * QUART], U16, name="xw_tail", align_bytes=64, offset=0)
        for q in range(2):
            lo = (2 + q) * QUART
            nc.vector.tensor_copy(
                xw_tail[:, q * QUART : (q + 1) * QUART],
                xw_win[:].indirect(l_tok[:, lo // LIST_COL : (lo + QUART) // LIST_COL]),
            )

        def words(lo, hi):
            return xw_head[:, lo:hi] if hi <= 2 * QUART else xw_tail[:, lo - 2 * QUART : hi - 2 * QUART]

        a_tiles = []
        for t in range(PACK):
            if t > 0:
                matrix.append(quantise_matrix(t))
            codes, scales = matrix[t]
            a_t = keep.tile([P, J], F32, name=f"a{t}")
            width = QUART if t == 0 else BANK
            for lo in range(0, J, width):
                hi = lo + width
                acc = next_bank([P, width], f"acc{t}_{lo}")
                nc.tensor.matmul_mx(
                    acc[:], lhsT=codes[:].bitcast(FP8X4), lhsT_scale=scales[:],
                    rhs=words(lo, hi).bitcast(FP4X4), rhs_scale=xs[:, lo:hi], start=True, stop=True,
                )
                if t == 0 and lo != 2 * QUART:
                    nc.scalar.copy(a_t[:, lo:hi], acc[:])
                else:
                    nc.vector.tensor_copy(a_t[:, lo:hi], acc[:])
            a_tiles.append(a_t)

        hid = keep.tile([P, PACK, O], BF16, name="hid", align_bytes=64)
        HALF = O // 2
        out_rows = out.rearrange("(b p) o -> p b o", p=P)

        def neighbours(t, lo, hi, part_tag, pieces):
            g = []
            for i in range(3):
                shares = (t, lo) in ((3, 0), (2, HALF))
                gi = keep.tile([P, hi - lo], F32, name=f"g{t}_{lo}_{i}", tag=f"g_shared{i}" if shares else f"g{t}_{lo}_{i}")
                nc.scalar.activation(
                    gi[:], a_tiles[t][:].indirect(l_slot[i][:, lo // LIST_COL : hi // LIST_COL]),
                    COPY, scale=slot_w[i][:, t : t + 1],
                )
                g.append(gi)
                if i == 1:
                    part = keep.tile([P, hi - lo], F32, name=f"part{t}_{lo}", tag=part_tag, align_bytes=64)
                    nc.vector.tensor_tensor(part[:], g[0][:], g[1][:], ADD)
            w = (hi - lo) // pieces
            for s in range(0, hi - lo, w):
                nc.vector.tensor_tensor(hid[:, t, lo + s : lo + s + w], part[:, s : s + w], g[2][:, s : s + w], ADD)

        def interleave_hidden(lo, hi, tag):
            grouped = keep.tile([P, hi - lo, PACK], BF16, name=f"hid_g{lo}", tag=tag, align_bytes=64)
            nc.vector.tensor_scalar_max(
                grouped[:].rearrange("p (c i) t -> p c t i", i=4),
                hid[:, :, lo:hi].rearrange("p t (c i) -> p c t i", i=4),
                0.0,
            )
            return grouped

        def quantise_hidden(grouped, lo, tag):
            width = grouped.shape[1]
            codes = keep.tile([P, width], U32, name=f"hid_c{lo}", tag=tag, align_bytes=64)
            scales = keep.tile([P, width], U8, name=f"hid_s{lo}", align_bytes=64)
            nc.vector.quantize_mx(codes[:].bitcast(FP8X4), scales[:], grouped[:].rearrange("p o t -> p (o t)"))
            return codes, scales

        def second_product(codes, scales, lo, engines):
            width = codes.shape[1]
            y = keep.tile([P, N // P, width], F32, name=f"y_sb{lo}")
            last = lo + width == O
            for b in range(N // P):
                acc = next_bank([P, width], f"y{lo}_{b}")
                nc.tensor.matmul_mx(
                    acc[:], lhsT=wb_w[:, 2 * P * b : 2 * P * (b + 1)].bitcast(FP4X4), lhsT_scale=wb_s[:, P * b : P * (b + 1)],
                    rhs=codes[:].bitcast(FP8X4), rhs_scale=scales[:], start=True, stop=True,
                )
                if engines[b] == "scalar":
                    nc.scalar.copy(y[:, b, :], acc[:])
                else:
                    nc.vector.tensor_copy(y[:, b, :], acc[:])
                if last:
                    queue = nc.scalar if engines[b] == "scalar" else nc.sync
                    queue.dma_start(out_rows[:, b, lo : lo + width], y[:, b, :])
            if not last:
                nc.sync.dma_start(out_rows[:, :, lo : lo + width], y[:])

        neighbours(0, 0, O, "part_a", 1)
        neighbours(1, 0, O, "part_b", 1)
        neighbours(2, 0, HALF, "part_a", 1)
        neighbours(3, 0, HALF, "part_b", 1)
        codes, scales = quantise_hidden(interleave_hidden(0, HALF, "hid_g0"), 0, "codes0")
        second_product(codes, scales, 0, ("scalar", "scalar"))
        neighbours(3, HALF, O, "part_a", 1)
        neighbours(2, HALF, O, "part_b", 2)
        starts = (HALF, HALF + HALF // 2)
        grouped = [interleave_hidden(lo, lo + HALF // 2, f"hid_g{lo}") for lo in starts]
        quantised = [quantise_hidden(g, lo, f"codes{lo}") for g, lo in zip(grouped, starts)]
        second_product(*quantised[0], starts[0], ("scalar", "scalar"))
        second_product(*quantised[1], starts[1], ("scalar", "vector"))
